import numpy as np
import ml_dtypes


def mxq(x, axis, fmt="e4m3"):
    dtype, down = {"e4m3": (ml_dtypes.float8_e4m3fn, 7), "e5m2": (ml_dtypes.float8_e5m2, 14)}[fmt]
    v = np.moveaxis(np.asarray(x, np.float32).astype(ml_dtypes.bfloat16).astype(np.float64), axis, -1)
    blocks = v.reshape(v.shape[:-1] + (-1, 32))
    amax = np.abs(blocks).max(-1, keepdims=True)
    byte = np.maximum(np.where(amax > 0, np.frexp(amax)[1] - 1 + 127, 0) - down, 1)
    scale = np.exp2(byte - 127.0)
    codes = (blocks / scale).astype(np.float32).astype(dtype).astype(np.float64)
    return np.moveaxis((codes * scale).reshape(v.shape), -1, axis)


WIDE = False


def mx_kscale(k):
    if not WIDE:
        return np.ones(k)
    levels = np.array([10, -10, 5, -5, 0])
    if k % 512:
        return np.exp2(np.random.permutation(np.resize(levels, k // 32))).repeat(32)
    a = np.empty((k // 512, 16))
    for p in range(k // 512):
        a[p, :8] = np.random.permutation(np.resize(levels, 8))
        for g in range(8):
            far = levels[np.abs(levels - a[p, g]) >= 10]
            a[p, g + 8] = far[np.random.randint(len(far))]
    return np.exp2(a.ravel()).repeat(32)


def f64(x):
    return np.asarray(x).astype(np.float64)


def striped(idx):
    return np.tile(idx.reshape(-1, 16).T, (8, 1)).astype(np.uint16)


def unstriped(offs):
    return offs[:16].T.reshape(-1).astype(np.int64)


def pack_weight(w):
    k, n = w.shape
    w = f64(np.asarray(w, np.float32).astype(ml_dtypes.bfloat16)).reshape(k // 32, 32, n)
    amax = np.abs(w).max(1)
    byte = np.clip(np.where(amax > 0, np.frexp(amax)[1] - 1 + 127 - 7, 1), 1, 254)
    scaled = (w * np.exp2(127.0 - byte)[:, None, :]).reshape(k, n).astype(np.float32)
    words = np.ascontiguousarray(scaled.reshape(k // 512, 128, 4, n).transpose(0, 1, 3, 2)).astype(ml_dtypes.float8_e4m3fn).view(np.uint8)
    return words, np.ascontiguousarray(byte.astype(np.uint8).reshape(k // 512, 16, n))


def unpack_weight(words, scales):
    g, p, n, _ = words.shape
    vals = np.ascontiguousarray(words).view(ml_dtypes.float8_e4m3fn).astype(np.float64) * np.repeat(np.exp2(scales.astype(np.float64) - 127.0), 8, axis=1)[..., None]
    return vals.transpose(0, 1, 3, 2).reshape(g * 512, n)


def sigmoid(v):
    return 1.0 / (1.0 + np.exp(-np.maximum(v, -700.0)))


K, T, S, N = 512, 2048, 512, 128
P = 2 ** 7


def setup_inputs():
    n = np.random.standard_normal
    s = mx_kscale(K)[:, None]
    packed_xT = pack_weight(n((K, T)) * s)
    return {
        "x_words": packed_xT[0],
        "x_scales": packed_xT[1],
        "w1": (n((K, N)) / np.sqrt(K) / s).astype(np.float32),
        "w2": (n((K, N)) / np.sqrt(K) / s).astype(np.float32),
        "offset": (np.tile(0.5 * n(S), (P, 1))).astype(np.float32),
        "lab": (np.tile((np.random.uniform(size=S) < 0.5) * 1.0, (P, 1))).astype(np.float32),
        "brier": (np.random.uniform(0.2, 0.8, (N, 1))).astype(np.float32),
        "offs": striped(np.random.permutation(T)[:S]),
    }


def reference(x_words, x_scales, w1, w2, offset, lab, brier, offs):
    xq = unpack_weight(x_words, x_scales)[:, unstriped(offs)]
    ym = mxq(f64(w1), 0, "e4m3").T @ xq
    ys = mxq(f64(w2), 0, "e4m3").T @ xq
    sd = 0.8 * (np.log(np.exp(ys) + 1.0)) + 0.3
    s0 = sigmoid(ym + f64(offset)[:1] + -2.3344 * sd)
    s1 = sigmoid(ym + f64(offset)[:1] + -0.7420 * sd)
    s2 = sigmoid(ym + f64(offset)[:1] + 0.7420 * sd)
    s3 = sigmoid(ym + f64(offset)[:1] + 2.3344 * sd)
    pm = 0.0459 * s0 + 0.4541 * s1 + 0.4541 * s2 + 0.0459 * s3
    return (0.0459 * (s0 * (-1.0 * s0 + 1.0)) + 0.4541 * (s1 * (-1.0 * s1 + 1.0)) + 0.4541 * (s2 * (-1.0 * s2 + 1.0)) + 0.0459 * (s3 * (-1.0 * s3 + 1.0))) / (pm * (-1.0 * pm + 1.0) + 0.02) - (f64(brier) * ((pm - f64(lab)[:1]) ** 2))

@@ -1,0 +1,200 @@
+import math
+from contextlib import ExitStack
+
+import concourse.mybir as mybir
+from concourse.masks import make_identity
+
+K, T, S, N = 512, 2048, 512, 128
+FLOPS = 2 * 2 * K * S * N
+
+F32 = mybir.dt.float32
+BF16 = mybir.dt.bfloat16
+I32 = mybir.dt.int32
+U32 = mybir.dt.uint32
+U16 = mybir.dt.uint16
+U8 = mybir.dt.uint8
+FP8X4 = mybir.dt.float8_e4m3fn_x4
+ALU = mybir.AluOpType
+ACT = mybir.ActivationFunctionType
+
+P = 128
+PACK = 4
+BLOCKS = S // P
+HALVES = 2
+PER = BLOCKS // HALVES
+WIDE = PER * P
+
+NODES = (2.3344, 0.7420)
+WEIGHTS = (0.0459, 0.4541)
+WSUM = 0.0459 + 0.4541 + 0.4541 + 0.0459
+
+SP_AMP = (-1.2762599117001776, -0.5435210914270948, -0.2205511065976243)
+SP_SLOPE = (0.5012841530723693, 0.4992542937611325, 0.5002126802985076)
+SP_SHIFT = (1.2838935200381207, 0.45991611173218133, 0.08656906098645972)
+SP_BASE = 2.040332108721264
+
+
+def tile_picked_yghqlr_var_p_kernel(tc, x_words, x_scales, w1, w2, offset, lab, brier, offs, out):
+    nc = tc.nc
+    with ExitStack() as ctx:
+        keep = ctx.enter_context(tc.tile_pool(name="keep", bufs=1))
+        psum = ctx.enter_context(tc.psum_pool(name="psum", bufs=1))
+
+        def bank(i, name):
+            return psum.tile([P, 512], F32, tag="bank%d" % i, name=name)
+
+        def work(name, width=WIDE):
+            return keep.tile([P, width], F32, name=name, align_bytes=64)
+
+        offsets = keep.tile([P, S // 16], U16, name="offsets")
+        nc.sync.dma_start(offsets[:], offs)
+
+        scale_tab = keep.tile([P, T], U8, name="scale_tab", align_bytes=64)
+        nc.vector.memset(scale_tab[:].bitcast(I32), 0)
+        for q in range(4):
+            nc.scalar.dma_start(out=scale_tab[32 * q : 32 * q + 4, :].bitcast(I32), in_=x_scales[0, 4 * q : 4 * q + 4, :].bitcast(I32))
+
+        raw = []
+        for i, w in enumerate((w2, w1)):
+            r = keep.tile([P, PACK, N], F32, name="raw%d" % i)
+            nc.sync.dma_start(out=r[:], in_=w.rearrange("(p j) n -> p j n", j=PACK))
+            raw.append(r)
+        word_tab = keep.tile([P, T], I32, name="word_tab", align_bytes=64)
+        nc.sync.dma_start(out=word_tab[:], in_=x_words[0].rearrange("p n t -> p (n t)").bitcast(I32))
+
+        rows = keep.tile([P, P], F32, name="rows")
+        nc.gpsimd.memset(rows[:], 0.0)
+        ident = keep.tile([P, P], F32, name="ident")
+        make_identity(nc, ident[:])
+        nc.scalar.dma_start(out=rows[0:BLOCKS, :], in_=offset[0].rearrange("(b p) -> b p", p=P))
+        nc.scalar.dma_start(out=rows[BLOCKS : 2 * BLOCKS, :], in_=lab[0].rearrange("(b p) -> b p", p=P))
+        nc.scalar.dma_start(out=rows[2 * BLOCKS : 2 * BLOCKS + 1, :], in_=brier.rearrange("p o -> o p"))
+
+        x_scale = keep.tile([P, S], U8, name="x_scale", align_bytes=64)
+        nc.vector.tensor_copy(x_scale[:], scale_tab[:].indirect(offsets[:]))
+
+        grouped = keep.tile([P, 2, N, PACK], BF16, name="grouped", align_bytes=64)
+        for i in range(2):
+            nc.vector.tensor_copy(out=grouped[:, i], in_=raw[i][:].rearrange("p j n -> p n j"))
+        w_codes = keep.tile([P, 2 * N], U32, name="w_codes", align_bytes=64)
+        w_scale = keep.tile([P, 2 * N], U8, name="w_scale", align_bytes=64)
+        nc.vector.quantize_mx(out=w_codes[:].bitcast(FP8X4), scales=w_scale[:], in_=grouped[:].rearrange("p i n j -> p (i n j)"))
+
+        cols = bank(7, "cols")
+        nc.tensor.transpose(cols[:, 0:P], rows[:], ident[:])
+        off_col = keep.tile([P, BLOCKS], F32, name="off_col")
+        flip_col = keep.tile([P, BLOCKS], F32, name="flip_col")
+        neg_brier = keep.tile([P, 1], F32, name="neg_brier")
+        nc.scalar.copy(off_col[:], cols[:, 0:BLOCKS])
+        nc.scalar.activation(flip_col[:], cols[:, BLOCKS : 2 * BLOCKS], ACT.Identity, bias=1.0, scale=-2.0)
+        nc.scalar.activation(neg_brier[:], cols[:, 2 * BLOCKS : 2 * BLOCKS + 1], ACT.Identity, scale=-1.0)
+
+        ys, ym = [], []
+        for h in range(HALVES):
+            codes = keep.tile([P, WIDE], U32, name="x_codes%d" % h, align_bytes=64)
+            nc.vector.tensor_copy(codes[:], word_tab[:].bitcast(U32).indirect(offsets[:, h * WIDE // 16 : (h + 1) * WIDE // 16]))
+            for i, banks in enumerate((ys, ym)):
+                acc = bank(2 * h + i, "acc%d_%d" % (h, i))
+                banks.append(acc)
+                for b in range(PER):
+                    j0 = h * WIDE + b * P
+                    nc.tensor.matmul_mx(
+                        out=acc[:, b * P : (b + 1) * P],
+                        lhsT=codes[:, b * P : (b + 1) * P].bitcast(FP8X4),
+                        lhsT_scale=x_scale[:, j0 : j0 + P],
+                        rhs=w_codes[:, i * N : (i + 1) * N].bitcast(FP8X4),
+                        rhs_scale=w_scale[:, i * N : (i + 1) * N],
+                        start=True,
+                        stop=True,
+                    )
+
+        soft, mean = [], []
+        for h in range(HALVES):
+            mag = work("mag%d" % h)
+            nc.scalar.activation(mag[:], ys[h][:, 0:WIDE], ACT.Abs)
+            acc = work("relu%d" % h)
+            nc.scalar.activation(acc[:], ys[h][:, 0:WIDE], ACT.Relu)
+            a = work("mean%d" % h)
+            for b in range(PER):
+                c = h * PER + b
+                nc.vector.tensor_scalar(a[:, b * P : (b + 1) * P], ym[h][:, b * P : (b + 1) * P], off_col[:, c : c + 1], flip_col[:, c : c + 1], ALU.add, ALU.mult)
+            mean.append(a)
+            for i in range(3):
+                g = work("g%d_%d" % (h, i))
+                nc.scalar.activation(g[:], mag[:], ACT.Tanh, bias=SP_SHIFT[i], scale=SP_SLOPE[i])
+                nxt = work("soft%d_%d" % (h, i))
+                nc.vector.scalar_tensor_tensor(nxt[:], g[:], SP_AMP[i], acc[:], ALU.mult, ALU.add)
+                acc = nxt
+            soft.append(acc)
+
+        half_w = 0.5 * WEIGHTS[1]
+        lift = (0.5 * WSUM + 0.02) / half_w
+        terms = [(node, sign) for node in range(2) for sign in (1.0, -1.0)]
+        tanhs, tsum = [], []
+        for h in range(HALVES):
+            ts, addends = [], []
+            for i, (node, sign) in enumerate(terms):
+                c = sign * NODES[node]
+                u = work("u%d_%d" % (h, i))
+                nc.vector.scalar_tensor_tensor(u[:], soft[h][:], 0.8 * c, mean[h][:], ALU.mult, ALU.add)
+                t = work("t%d_%d" % (h, i))
+                nc.scalar.activation(t[:], u[:], ACT.Tanh, bias=0.5 * c * (0.8 * SP_BASE + 0.3), scale=0.5)
+                ts.append(t)
+            for i, (node, sign) in enumerate(terms):
+                if node == 0:
+                    s = work("ts%d_%d" % (h, i))
+                    nc.vector.tensor_scalar(s[:], ts[i][:], WEIGHTS[0] / WEIGHTS[1], 0.5 * lift, ALU.mult, ALU.add)
+                    addends.append(s)
+                else:
+                    addends.append(ts[i])
+            banks = [bank((4, 5, 0, 1)[h * PER + b], "tsum%d_%d" % (h, b)) for b in range(PER)]
+            for i in range(4):
+                for b in range(PER):
+                    nc.tensor.matmul(banks[b][:, 0:P], addends[i][:, b * P : (b + 1) * P], ident[:], start=(i == 0), stop=(i == 3), is_transpose=True)
+            tanhs.append(ts)
+            tsum.append(banks)
+
+        sq_mean, den, qsum = [], [], []
+        for h in range(HALVES):
+            g = work("pm2_%d" % h)
+            d = work("den%d" % h)
+            for b in range(PER):
+                nc.scalar.activation(g[:, b * P : (b + 1) * P], tsum[h][b][:, 0:P], ACT.Square, bias=-0.02, scale=half_w)
+            for b in range(PER):
+                nc.vector.scalar_tensor_tensor(d[:, b * P : (b + 1) * P], tsum[h][b][:, 0:P], -half_w, g[:, b * P : (b + 1) * P], ALU.mult, ALU.add)
+            sq_mean.append(g)
+            den.append(d)
+            sqs = []
+            for i, (node, sign) in enumerate(terms):
+                sq = work("sq%d_%d" % (h, i))
+                nc.scalar.activation(sq[:], tanhs[h][i][:], ACT.Square, scale=0.5 * math.sqrt(WEIGHTS[node]))
+                sqs.append(sq)
+            q = bank((6, 2)[h], "qsum%d" % h)
+            for b in range(PER):
+                for i in range(4):
+                    nc.tensor.matmul(q[:, b * P : (b + 1) * P], sqs[i][:, b * P : (b + 1) * P], ident[:], start=(i == 0), stop=(i == 3), is_transpose=True)
+            qsum.append(q)
+
+        def two(ap):
+            return ap.rearrange("p (u c) -> p u c", u=2)
+
+        p1 = [work("p1_%d" % h, WIDE // 2) for h in range(HALVES)]
+        p2 = [work("p2_%d" % h, WIDE // 4) for h in range(HALVES)]
+        r2 = [work("r2_%d" % h, WIDE // 4) for h in range(HALVES)]
+        r1 = [work("r1_%d" % h, WIDE // 2) for h in range(HALVES)]
+        num = [work("num%d" % h) for h in range(HALVES)]
+        ratio = [work("ratio%d" % h) for h in range(HALVES)]
+        res = [work("res%d" % h) for h in range(HALVES)]
+        for h in range(HALVES):
+            nc.vector.tensor_tensor(p1[h][:], den[h][:, 0 : WIDE // 2], den[h][:, WIDE // 2 : WIDE], ALU.mult)
+        for h in range(HALVES):
+            nc.vector.tensor_tensor(p2[h][:], p1[h][:, 0 : WIDE // 4], p1[h][:, WIDE // 4 : WIDE // 2], ALU.mult)
+        for h in range(HALVES):
+            nc.vector.reciprocal(r2[h][:], p2[h][:])
+        for h in range(HALVES):
+            nc.vector.tensor_tensor(two(r1[h][:]), two(p1[h][:])[:, ::-1, :], r2[h][:].unsqueeze(1).to_broadcast([P, 2, WIDE // 4]), ALU.mult)
+        for h in range(HALVES):
+            nc.vector.scalar_tensor_tensor(two(num[h][:]), two(qsum[h][:, 0:WIDE]), 0.25 * WSUM, two(den[h][:])[:, ::-1, :], ALU.subtract, ALU.mult)
+            nc.vector.tensor_tensor(two(ratio[h][:]), two(num[h][:]), r1[h][:].unsqueeze(1).to_broadcast([P, 2, WIDE // 2]), ALU.mult)
+            nc.vector.scalar_tensor_tensor(res[h][:], sq_mean[h][:], neg_brier[:, 0:1], ratio[h][:], ALU.mult, ALU.add)
+            nc.sync.dma_start(out=out[:, h * WIDE : (h + 1) * WIDE], in_=res[h][:])

@@ -2,7 +2,6 @@ import math
 from contextlib import ExitStack
 
 import concourse.mybir as mybir
-from concourse.masks import make_identity
 
 K, T, S, N = 512, 2048, 512, 128
 FLOPS = 2 * 2 * K * S * N
@@ -20,9 +19,8 @@ ACT = mybir.ActivationFunctionType
 P = 128
 PACK = 4
 BLOCKS = S // P
-HALVES = 2
-PER = BLOCKS // HALVES
-WIDE = PER * P
+HALF = S // 2
+OPT = {"order":"a0 s0 C m0 a1 s1 m1 n0 t0 n1 t1 d0 d1 i0 i1 q0 p0 f0 q1 p1 f1","relu":"vv","den":"ss","sq":"SSSS","sbanks":[4,5,6,7],"tbanks":[0,1,4,5],"qbanks":[2,3,6,7]}
 
 NODES = (2.3344, 0.7420)
 WEIGHTS = (0.0459, 0.4541)
@@ -38,163 +36,279 @@ def tile_picked_yghqlr_var_p_kernel(tc, x_words, x_scales, w1, w2, offset, lab, 
     nc = tc.nc
     with ExitStack() as ctx:
         keep = ctx.enter_context(tc.tile_pool(name="keep", bufs=1))
+        late = ctx.enter_context(tc.tile_pool(name="late", bufs=1))
         psum = ctx.enter_context(tc.psum_pool(name="psum", bufs=1))
 
         def bank(i, name):
             return psum.tile([P, 512], F32, tag="bank%d" % i, name=name)
 
-        def work(name, width=WIDE):
-            return keep.tile([P, width], F32, name=name, align_bytes=64)
+        def work(name, width, tag=None):
+            return keep.tile([P, width], F32, name=name, tag=tag or name, align_bytes=64)
 
+        chunks = OPT.get("chunks", [[0, 1], [2, 3]])
         offsets = keep.tile([P, S // 16], U16, name="offsets")
         nc.sync.dma_start(offsets[:], offs)
 
-        scale_tab = keep.tile([P, T], U8, name="scale_tab", align_bytes=64)
-        nc.vector.memset(scale_tab[:].bitcast(I32), 0)
-        for q in range(4):
-            nc.scalar.dma_start(out=scale_tab[32 * q : 32 * q + 4, :].bitcast(I32), in_=x_scales[0, 4 * q : 4 * q + 4, :].bitcast(I32))
+        raw2 = keep.tile([P, PACK, N], F32, name="raw2")
+        nc.sync.dma_start(out=raw2[:], in_=w2.rearrange("(p j) n -> p j n", j=PACK))
 
-        raw = []
-        for i, w in enumerate((w2, w1)):
-            r = keep.tile([P, PACK, N], F32, name="raw%d" % i)
-            nc.sync.dma_start(out=r[:], in_=w.rearrange("(p j) n -> p j n", j=PACK))
-            raw.append(r)
-        word_tab = keep.tile([P, T], I32, name="word_tab", align_bytes=64)
+        ones = late.tile([P, P], F32, name="ones", offset=4 * T - 64, align_bytes=64)
+        nc.gpsimd.memset(ones[:], 1.0)
+        scale_tab = keep.tile([P, T], U8, name="scale_tab", align_bytes=64)
+        nc.gpsimd.memset(scale_tab[:].bitcast(I32), 0)
+        for q in range(4):
+            nc.sync.dma_start(out=scale_tab[32 * q : 32 * q + 4, :].bitcast(I32), in_=x_scales[0, 4 * q : 4 * q + 4, :].bitcast(I32))
+
+        ident = keep.tile([P, P], F32, name="ident")
+        nc.gpsimd.affine_select(out=ident[:], in_=ones[:], compare_op=ALU.is_equal, fill=0.0, base=0, pattern=[[-1, P]], channel_multiplier=1)
+        word_tab = late.tile([P, T], I32, name="word_tab", offset=0, align_bytes=64)
         nc.sync.dma_start(out=word_tab[:], in_=x_words[0].rearrange("p n t -> p (n t)").bitcast(I32))
+
+        raw1 = late.tile([P, PACK, N], F32, name="raw1", offset=4 * T + 4 * P - 128, align_bytes=64)
+        nc.sync.dma_start(out=raw1[:], in_=w1.rearrange("(p j) n -> p j n", j=PACK))
 
         rows = keep.tile([P, P], F32, name="rows")
         nc.gpsimd.memset(rows[:], 0.0)
-        ident = keep.tile([P, P], F32, name="ident")
-        make_identity(nc, ident[:])
-        nc.scalar.dma_start(out=rows[0:BLOCKS, :], in_=offset[0].rearrange("(b p) -> b p", p=P))
-        nc.scalar.dma_start(out=rows[BLOCKS : 2 * BLOCKS, :], in_=lab[0].rearrange("(b p) -> b p", p=P))
-        nc.scalar.dma_start(out=rows[2 * BLOCKS : 2 * BLOCKS + 1, :], in_=brier.rearrange("p o -> o p"))
+        nc.sync.dma_start(out=rows[0:BLOCKS, :], in_=offset[0].rearrange("(b p) -> b p", p=P))
+        nc.sync.dma_start(out=rows[32 : 32 + BLOCKS, :], in_=lab[0].rearrange("(b p) -> b p", p=P))
+        nc.sync.dma_start(out=rows[64:65, :], in_=brier.rearrange("p o -> o p"))
 
-        x_scale = keep.tile([P, S], U8, name="x_scale", align_bytes=64)
-        nc.vector.tensor_copy(x_scale[:], scale_tab[:].indirect(offsets[:]))
+        def quantised(raw, cast, name):
+            grouped = keep.tile([P, N, PACK], BF16, name=name + "_grouped", align_bytes=64)
+            cast(grouped[:], raw[:].rearrange("p j n -> p n j"))
+            codes = keep.tile([P, N], U32, name=name + "_codes", align_bytes=64)
+            scale = keep.tile([P, N], U8, name=name + "_scale", align_bytes=64)
+            nc.vector.quantize_mx(out=codes[:].bitcast(FP8X4), scales=scale[:], in_=grouped[:].rearrange("p n j -> p (n j)"))
+            return codes, scale
 
-        grouped = keep.tile([P, 2, N, PACK], BF16, name="grouped", align_bytes=64)
-        for i in range(2):
-            nc.vector.tensor_copy(out=grouped[:, i], in_=raw[i][:].rearrange("p j n -> p n j"))
-        w_codes = keep.tile([P, 2 * N], U32, name="w_codes", align_bytes=64)
-        w_scale = keep.tile([P, 2 * N], U8, name="w_scale", align_bytes=64)
-        nc.vector.quantize_mx(out=w_codes[:].bitcast(FP8X4), scales=w_scale[:], in_=grouped[:].rearrange("p i n j -> p (i n j)"))
+        w2q = quantised(raw2, nc.vector.tensor_copy, "w2")
 
-        cols = bank(7, "cols")
-        nc.tensor.transpose(cols[:, 0:P], rows[:], ident[:])
+        x_scale, x_codes = [], []
+        for h in range(2):
+            sc = keep.tile([P, HALF], U8, name="x_scale%d" % h, align_bytes=64)
+            nc.vector.tensor_copy(sc[:], scale_tab[:].indirect(offsets[:, h * HALF // 16 : (h + 1) * HALF // 16]))
+            x_scale.append(sc)
+        for h in range(2):
+            co = keep.tile([P, HALF], U32, name="x_codes%d" % h, align_bytes=64)
+            nc.vector.tensor_copy(co[:], word_tab[:].bitcast(U32).indirect(offsets[:, h * HALF // 16 : (h + 1) * HALF // 16]))
+            x_codes.append(co)
+
+        def product(acc, col, b, wq):
+            j0 = (b % 2) * P
+            nc.tensor.matmul_mx(
+                out=acc[:, col * P : (col + 1) * P],
+                lhsT=x_codes[b // 2][:, j0 : j0 + P].bitcast(FP8X4),
+                lhsT_scale=x_scale[b // 2][:, j0 : j0 + P],
+                rhs=wq[0][:].bitcast(FP8X4),
+                rhs_scale=wq[1][:],
+                start=True,
+                stop=True,
+            )
+
+        ys, ym = [], []
+        for h in range(2):
+            acc = bank(h, "ys%d" % h)
+            nc.tensor.matmul_mx(
+                out=acc[:, 0:HALF],
+                lhsT=w2q[0][:].bitcast(FP8X4),
+                lhsT_scale=w2q[1][:],
+                rhs=x_codes[h][:].bitcast(FP8X4),
+                rhs_scale=x_scale[h][:],
+                start=True,
+                stop=True,
+            )
+            ys.append(acc)
+        w1q = quantised(raw1, nc.scalar.copy if OPT.get("cast1", "s") == "s" else nc.vector.tensor_copy, "w1")
+        for h in range(2):
+            acc = bank(2 + h, "ym%d" % h)
+            for b in range(2):
+                product(acc, b, 2 * h + b, w1q)
+            ym.append(acc)
+            if h == 0:
+                cols = acc[:, HALF : HALF + P]
+                nc.tensor.transpose(cols, rows[:], ident[:])
         off_col = keep.tile([P, BLOCKS], F32, name="off_col")
         flip_col = keep.tile([P, BLOCKS], F32, name="flip_col")
         neg_brier = keep.tile([P, 1], F32, name="neg_brier")
-        nc.scalar.copy(off_col[:], cols[:, 0:BLOCKS])
-        nc.scalar.activation(flip_col[:], cols[:, BLOCKS : 2 * BLOCKS], ACT.Identity, bias=1.0, scale=-2.0)
-        nc.scalar.activation(neg_brier[:], cols[:, 2 * BLOCKS : 2 * BLOCKS + 1], ACT.Identity, scale=-1.0)
-
-        ys, ym = [], []
-        for h in range(HALVES):
-            codes = keep.tile([P, WIDE], U32, name="x_codes%d" % h, align_bytes=64)
-            nc.vector.tensor_copy(codes[:], word_tab[:].bitcast(U32).indirect(offsets[:, h * WIDE // 16 : (h + 1) * WIDE // 16]))
-            for i, banks in enumerate((ys, ym)):
-                acc = bank(2 * h + i, "acc%d_%d" % (h, i))
-                banks.append(acc)
-                for b in range(PER):
-                    j0 = h * WIDE + b * P
-                    nc.tensor.matmul_mx(
-                        out=acc[:, b * P : (b + 1) * P],
-                        lhsT=codes[:, b * P : (b + 1) * P].bitcast(FP8X4),
-                        lhsT_scale=x_scale[:, j0 : j0 + P],
-                        rhs=w_codes[:, i * N : (i + 1) * N].bitcast(FP8X4),
-                        rhs_scale=w_scale[:, i * N : (i + 1) * N],
-                        start=True,
-                        stop=True,
-                    )
-
-        soft, mean = [], []
-        for h in range(HALVES):
-            mag = work("mag%d" % h)
-            nc.scalar.activation(mag[:], ys[h][:, 0:WIDE], ACT.Abs)
-            acc = work("relu%d" % h)
-            nc.scalar.activation(acc[:], ys[h][:, 0:WIDE], ACT.Relu)
-            a = work("mean%d" % h)
-            for b in range(PER):
-                c = h * PER + b
-                nc.vector.tensor_scalar(a[:, b * P : (b + 1) * P], ym[h][:, b * P : (b + 1) * P], off_col[:, c : c + 1], flip_col[:, c : c + 1], ALU.add, ALU.mult)
-            mean.append(a)
-            for i in range(3):
-                g = work("g%d_%d" % (h, i))
-                nc.scalar.activation(g[:], mag[:], ACT.Tanh, bias=SP_SHIFT[i], scale=SP_SLOPE[i])
-                nxt = work("soft%d_%d" % (h, i))
-                nc.vector.scalar_tensor_tensor(nxt[:], g[:], SP_AMP[i], acc[:], ALU.mult, ALU.add)
-                acc = nxt
-            soft.append(acc)
-
-        half_w = 0.5 * WEIGHTS[1]
-        lift = (0.5 * WSUM + 0.02) / half_w
-        terms = [(node, sign) for node in range(2) for sign in (1.0, -1.0)]
-        tanhs, tsum = [], []
-        for h in range(HALVES):
-            ts, addends = [], []
-            for i, (node, sign) in enumerate(terms):
-                c = sign * NODES[node]
-                u = work("u%d_%d" % (h, i))
-                nc.vector.scalar_tensor_tensor(u[:], soft[h][:], 0.8 * c, mean[h][:], ALU.mult, ALU.add)
-                t = work("t%d_%d" % (h, i))
-                nc.scalar.activation(t[:], u[:], ACT.Tanh, bias=0.5 * c * (0.8 * SP_BASE + 0.3), scale=0.5)
-                ts.append(t)
-            for i, (node, sign) in enumerate(terms):
-                if node == 0:
-                    s = work("ts%d_%d" % (h, i))
-                    nc.vector.tensor_scalar(s[:], ts[i][:], WEIGHTS[0] / WEIGHTS[1], 0.5 * lift, ALU.mult, ALU.add)
-                    addends.append(s)
-                else:
-                    addends.append(ts[i])
-            banks = [bank((4, 5, 0, 1)[h * PER + b], "tsum%d_%d" % (h, b)) for b in range(PER)]
-            for i in range(4):
-                for b in range(PER):
-                    nc.tensor.matmul(banks[b][:, 0:P], addends[i][:, b * P : (b + 1) * P], ident[:], start=(i == 0), stop=(i == 3), is_transpose=True)
-            tanhs.append(ts)
-            tsum.append(banks)
-
-        sq_mean, den, qsum = [], [], []
-        for h in range(HALVES):
-            g = work("pm2_%d" % h)
-            d = work("den%d" % h)
-            for b in range(PER):
-                nc.scalar.activation(g[:, b * P : (b + 1) * P], tsum[h][b][:, 0:P], ACT.Square, bias=-0.02, scale=half_w)
-            for b in range(PER):
-                nc.vector.scalar_tensor_tensor(d[:, b * P : (b + 1) * P], tsum[h][b][:, 0:P], -half_w, g[:, b * P : (b + 1) * P], ALU.mult, ALU.add)
-            sq_mean.append(g)
-            den.append(d)
-            sqs = []
-            for i, (node, sign) in enumerate(terms):
-                sq = work("sq%d_%d" % (h, i))
-                nc.scalar.activation(sq[:], tanhs[h][i][:], ACT.Square, scale=0.5 * math.sqrt(WEIGHTS[node]))
-                sqs.append(sq)
-            q = bank((6, 2)[h], "qsum%d" % h)
-            for b in range(PER):
-                for i in range(4):
-                    nc.tensor.matmul(q[:, b * P : (b + 1) * P], sqs[i][:, b * P : (b + 1) * P], ident[:], start=(i == 0), stop=(i == 3), is_transpose=True)
-            qsum.append(q)
 
         def two(ap):
             return ap.rearrange("p (u c) -> p u c", u=2)
 
-        p1 = [work("p1_%d" % h, WIDE // 2) for h in range(HALVES)]
-        p2 = [work("p2_%d" % h, WIDE // 4) for h in range(HALVES)]
-        r2 = [work("r2_%d" % h, WIDE // 4) for h in range(HALVES)]
-        r1 = [work("r1_%d" % h, WIDE // 2) for h in range(HALVES)]
-        num = [work("num%d" % h) for h in range(HALVES)]
-        ratio = [work("ratio%d" % h) for h in range(HALVES)]
-        res = [work("res%d" % h) for h in range(HALVES)]
-        for h in range(HALVES):
-            nc.vector.tensor_tensor(p1[h][:], den[h][:, 0 : WIDE // 2], den[h][:, WIDE // 2 : WIDE], ALU.mult)
-        for h in range(HALVES):
-            nc.vector.tensor_tensor(p2[h][:], p1[h][:, 0 : WIDE // 4], p1[h][:, WIDE // 4 : WIDE // 2], ALU.mult)
-        for h in range(HALVES):
-            nc.vector.reciprocal(r2[h][:], p2[h][:])
-        for h in range(HALVES):
-            nc.vector.tensor_tensor(two(r1[h][:]), two(p1[h][:])[:, ::-1, :], r2[h][:].unsqueeze(1).to_broadcast([P, 2, WIDE // 4]), ALU.mult)
-        for h in range(HALVES):
-            nc.vector.scalar_tensor_tensor(two(num[h][:]), two(qsum[h][:, 0:WIDE]), 0.25 * WSUM, two(den[h][:])[:, ::-1, :], ALU.subtract, ALU.mult)
-            nc.vector.tensor_tensor(two(ratio[h][:]), two(num[h][:]), r1[h][:].unsqueeze(1).to_broadcast([P, 2, WIDE // 2]), ALU.mult)
-            nc.vector.scalar_tensor_tensor(res[h][:], sq_mean[h][:], neg_brier[:, 0:1], ratio[h][:], ALU.mult, ALU.add)
-            nc.sync.dma_start(out=out[:, h * WIDE : (h + 1) * WIDE], in_=res[h][:])
+        half_w = 0.5 * WEIGHTS[1]
+        lift = (0.5 * WSUM + 0.02) / half_w
+        st = [dict() for c in chunks]
+        sbanks = OPT.get("sbanks", [4, 4, 5, 5])
+        tbanks = OPT.get("tbanks", [6, 7, 0, 1])
+        qbanks = OPT.get("qbanks", [2, 2, 3, 3])
+
+        def view(banks, c):
+            b0 = chunks[c][0]
+            return banks[b0 // 2][:, (b0 % 2) * P : (b0 % 2 + len(chunks[c])) * P]
+
+        def magnitude(c):
+            w = len(chunks[c]) * P
+            st[c]["mag"] = work("mag%d" % c, w)
+            nc.scalar.activation(st[c]["mag"][:], view(ys, c), ACT.Abs)
+            st[c]["acc"] = work("relu%d" % c, w)
+            if OPT.get("relu", "vvvv")[c] == "v":
+                nc.vector.tensor_scalar(st[c]["acc"][:], view(ys, c), 0.0, -1.0 / SP_AMP[0], ALU.max, ALU.mult)
+            else:
+                nc.scalar.activation(st[c]["acc"][:], view(ys, c), ACT.Relu, scale=-1.0 / SP_AMP[0])
+
+        def columns():
+            nc.vector.tensor_copy(off_col[:], cols[:, 0:BLOCKS])
+            nc.vector.tensor_scalar(flip_col[:], cols[:, 32 : 32 + BLOCKS], -2.0, 1.0, ALU.mult, ALU.add)
+            nc.vector.tensor_scalar(neg_brier[:], cols[:, 64:65], -1.0, None, ALU.mult)
+
+        def mean(c):
+            a = work("mean%d" % c, len(chunks[c]) * P)
+            for i, b in enumerate(chunks[c]):
+                nc.vector.tensor_scalar(a[:, i * P : (i + 1) * P], ym[b // 2][:, (b % 2) * P : (b % 2 + 1) * P], off_col[:, b : b + 1], flip_col[:, b : b + 1], ALU.add, ALU.mult)
+            st[c]["mean"] = a
+
+        def softplus(c):
+            w = len(chunks[c]) * P
+            addends = [st[c]["acc"][:]]
+            for i in (2, 1, 0):
+                g = work("g%d_%d" % (c, i), w)
+                nc.scalar.activation(g[:], st[c]["mag"][:], ACT.Tanh, bias=-SP_SHIFT[i], scale=-SP_SLOPE[i])
+                if i:
+                    s = work("gs%d_%d" % (c, i), w)
+                    nc.vector.tensor_scalar(s[:], g[:], SP_AMP[i] / SP_AMP[0], None, ALU.mult)
+                    g = s
+                addends.append(g[:])
+            st[c]["ssum"] = summed(c, addends, sbanks, "ssum")
+
+        def nodes(c):
+            w = len(chunks[c]) * P
+            ts = []
+            for node in range(2):
+                u = work("u%d_%d" % (c, node), 2 * w)
+                t = work("t%d_%d" % (c, node), 2 * w)
+                for i, sign in enumerate((1.0, -1.0)):
+                    for ps, sl in st[c]["ssum"]:
+                        nc.vector.scalar_tensor_tensor(u[:, i * w : (i + 1) * w][:, sl], ps, -0.8 * SP_AMP[0] * sign * NODES[node], st[c]["mean"][:, sl], ALU.mult, ALU.add)
+                    nc.scalar.activation(t[:, i * w : (i + 1) * w], u[:, i * w : (i + 1) * w], ACT.Tanh, bias=0.5 * sign * NODES[node] * (0.8 * SP_BASE + 0.3), scale=0.5)
+                ts.append(t)
+            st[c]["t"] = ts
+
+        def summed(c, addends, ids, name):
+            w = len(chunks[c]) * P
+            tiles = {}
+            for b in chunks[c]:
+                if ids[b] not in tiles:
+                    tiles[ids[b]] = bank(ids[b], "%s%d_%d" % (name, c, b))
+            shared = len(tiles) == 1
+            outs = [tiles[ids[b]][:, (i * P if shared else 0) : (i * P if shared else 0) + P] for i, b in enumerate(chunks[c])]
+            order = [(i, k) for i in range(len(outs)) for k in range(4)] if shared else [(i, k) for k in range(4) for i in range(len(outs))]
+            for i, k in order:
+                nc.tensor.matmul(outs[i], addends[k][:, i * P : (i + 1) * P], ident[:], start=(k == 0), stop=(k == 3), is_transpose=True)
+            if shared:
+                return [(tiles[ids[chunks[c][0]]][:, 0:w], slice(0, w))]
+            return [(outs[i], slice(i * P, (i + 1) * P)) for i in range(len(outs))]
+
+        def tsum(c):
+            w = len(chunks[c]) * P
+            s = work("ts%d" % c, 2 * w)
+            if OPT.get("ts", "vvvv")[c] == "v":
+                nc.vector.tensor_scalar(s[:], st[c]["t"][0][:], WEIGHTS[0] / WEIGHTS[1], 0.5 * lift, ALU.mult, ALU.add)
+            elif OPT.get("ts")[c] == "g":
+                nc.gpsimd.tensor_scalar(s[:], st[c]["t"][0][:], WEIGHTS[0] / WEIGHTS[1], 0.5 * lift, ALU.mult, ALU.add)
+            else:
+                nc.scalar.activation(s[:], st[c]["t"][0][:], ACT.Identity, bias=0.5 * lift, scale=WEIGHTS[0] / WEIGHTS[1])
+            st[c]["tsum"] = summed(c, [x[:, k * w : (k + 1) * w] for x in (s, st[c]["t"][1]) for k in range(2)], tbanks, "tsum")
+
+        def square(c, node):
+            w = len(chunks[c]) * P
+            sq = work("sq%d_%d" % (c, node), 2 * w, OPT.get("sqtag", {}).get("%d%d" % (c, node)))
+            t = st[c]["t"][node]
+            mode = OPT.get("sq", "ssssssss")[2 * c + node]
+            for sl in [slice(0, 2 * w)] if mode in "sv" else [slice(0, w), slice(w, 2 * w)]:
+                if mode in "sS":
+                    nc.scalar.activation(sq[:, sl], t[:, sl], ACT.Square, scale=0.5 * math.sqrt(WEIGHTS[node]))
+                else:
+                    nc.vector.scalar_tensor_tensor(sq[:, sl], t[:, sl], 0.25 * WEIGHTS[node], t[:, sl], ALU.mult, ALU.mult)
+            st[c]["sq%d" % node] = sq
+
+        def squares(c):
+            w = len(chunks[c]) * P
+            for node in range(2):
+                if "sq%d" % node not in st[c]:
+                    square(c, node)
+            sqs = [st[c]["sq0"], st[c]["sq1"]]
+            st[c]["qsum"] = summed(c, [x[:, k * w : (k + 1) * w] for x in sqs for k in range(2)], qbanks, "qsum")
+
+        def denominator(c):
+            w = len(chunks[c]) * P
+            g = work("pm2_%d" % c, w)
+            d = work("den%d" % c, w)
+            if OPT.get("den", "vvvv")[c] == "v":
+                for ps, sl in st[c]["tsum"]:
+                    nc.scalar.activation(g[:, sl], ps, ACT.Square, bias=-0.02, scale=half_w)
+                for ps, sl in st[c]["tsum"]:
+                    nc.vector.scalar_tensor_tensor(d[:, sl], ps, -half_w, g[:, sl], ALU.mult, ALU.add)
+            else:
+                e = work("dev%d" % c, w)
+                for ps, sl in st[c]["tsum"]:
+                    nc.scalar.activation(e[:, sl], ps, ACT.Square, bias=-0.52, scale=half_w)
+                nc.vector.tensor_scalar(d[:], e[:], 0.27, None, ALU.subtract)
+                st[c]["late"] = True
+            st[c]["g"] = g
+            st[c]["den"] = d
+
+        def penalty(c):
+            if "late" in st[c]:
+                for ps, sl in st[c]["tsum"]:
+                    nc.scalar.activation(st[c]["g"][:, sl], ps, ACT.Square, bias=-0.02, scale=half_w)
+
+        def inverse(c):
+            w = len(chunks[c]) * P
+            depth = OPT.get("depth", [2] * 4)[c]
+            prods = [st[c]["den"]]
+            for lv in range(1, depth + 1):
+                p = work("p%d_%d" % (lv, c), w >> lv)
+                nc.vector.tensor_tensor(p[:], prods[-1][:, 0 : w >> lv], prods[-1][:, w >> lv : w >> (lv - 1)], ALU.mult)
+                prods.append(p)
+            r = work("r%d_%d" % (depth, c), w >> depth)
+            nc.vector.reciprocal(r[:], prods[depth][:])
+            for lv in range(depth - 1, 0, -1):
+                nr = work("r%d_%d" % (lv, c), w >> lv)
+                nc.vector.tensor_tensor(two(nr[:]), two(prods[lv][:])[:, ::-1, :], r[:].unsqueeze(1).to_broadcast([P, 2, w >> (lv + 1)]), ALU.mult)
+                r = nr
+            st[c]["r"] = r
+
+        def finish(c):
+            w = len(chunks[c]) * P
+            j0 = chunks[c][0] * P
+            if OPT.get("fold", "nnnn")[c] == "y":
+                pen = work("pen%d" % c, w)
+                nc.vector.scalar_tensor_tensor(pen[:], st[c]["g"][:], neg_brier[:, 0:1], st[c]["den"][:], ALU.mult, ALU.mult)
+                top = work("top%d" % c, w)
+                for ps, sl in st[c]["qsum"]:
+                    nc.vector.scalar_tensor_tensor(top[:, sl], ps, 0.25 * WSUM, pen[:, sl], ALU.subtract, ALU.add)
+                num = work("num%d" % c, w)
+                nc.vector.tensor_tensor(two(num[:]), two(top[:]), two(st[c]["den"][:])[:, ::-1, :], ALU.mult)
+                res = work("res%d" % c, w)
+                nc.vector.tensor_tensor(two(res[:]), two(num[:]), st[c]["r"][:].unsqueeze(1).to_broadcast([P, 2, w // 2]), ALU.mult)
+                nc.sync.dma_start(out=out[:, j0 : j0 + w], in_=res[:])
+                return
+            num = work("num%d" % c, w)
+            swapped = two(st[c]["den"][:])[:, ::-1, :]
+            if len(st[c]["qsum"]) == 1:
+                nc.vector.scalar_tensor_tensor(two(num[:]), two(st[c]["qsum"][0][0]), 0.25 * WSUM, swapped, ALU.subtract, ALU.mult)
+            else:
+                for i, (ps, sl) in enumerate(st[c]["qsum"]):
+                    nc.vector.scalar_tensor_tensor(num[:, sl], ps, 0.25 * WSUM, swapped[:, i, :], ALU.subtract, ALU.mult)
+            ratio = work("ratio%d" % c, w)
+            nc.vector.tensor_tensor(two(ratio[:]), two(num[:]), st[c]["r"][:].unsqueeze(1).to_broadcast([P, 2, w // 2]), ALU.mult)
+            res = work("res%d" % c, w)
+            nc.vector.scalar_tensor_tensor(res[:], st[c]["g"][:], neg_brier[:, 0:1], ratio[:], ALU.mult, ALU.add)
+            j0 = chunks[c][0] * P
+            nc.sync.dma_start(out=out[:, j0 : j0 + w], in_=res[:])
+
+        steps = {"a": magnitude, "m": mean, "s": softplus, "n": nodes, "t": tsum, "q": squares, "d": denominator, "i": inverse, "f": finish, "p": penalty, "x": lambda c: square(c, 0), "y": lambda c: square(c, 1)}
+        for word in OPT.get("order", "a0 s0 C m0 a1 m1 s1 n0 t0 n1 t1 d0 q0 d1 q1 i0 i1 f0 f1").split():
+            if word == "C":
+                columns()
+            else:
+                steps[word[0]](int(word[1]))

@@ -20,7 +20,7 @@ P = 128
 PACK = 4
 BLOCKS = S // P
 HALF = S // 2
-OPT = {"order":"a0 s0 C m0 a1 s1 m1 n0 t0 n1 t1 d0 d1 i0 i1 q0 p0 f0 q1 p1 f1","relu":"vv","den":"ss","sq":"SSSS","sbanks":[4,5,6,7],"tbanks":[0,1,4,5],"qbanks":[2,3,6,7]}
+OPT = {"order":"a0 s0 C m0 a1 s1 m1 n0 t0 d0 n1 t1 d1 i0 i1 r0 r1 q0 q1 p0 p1 f0 f1","relu":"vv","den":"ss","sq":"vvvv","pen":"vv","inv":"ss","sbanks":[4,5,6,6],"tbanks":[0,1,4,5],"qbanks":[2,2,3,7]}
 
 NODES = (2.3344, 0.7420)
 WEIGHTS = (0.0459, 0.4541)
@@ -135,7 +135,7 @@ def tile_picked_yghqlr_var_p_kernel(tc, x_words, x_scales, w1, w2, offset, lab, 
             return ap.rearrange("p (u c) -> p u c", u=2)
 
         half_w = 0.5 * WEIGHTS[1]
-        lift = (0.5 * WSUM + 0.02) / half_w
+        lift = (0.5 * WSUM - 0.25) / half_w
         st = [dict() for c in chunks]
         sbanks = OPT.get("sbanks", [4, 4, 5, 5])
         tbanks = OPT.get("tbanks", [6, 7, 0, 1])
@@ -240,73 +240,64 @@ def tile_picked_yghqlr_var_p_kernel(tc, x_words, x_scales, w1, w2, offset, lab, 
 
         def denominator(c):
             w = len(chunks[c]) * P
-            g = work("pm2_%d" % c, w)
             d = work("den%d" % c, w)
-            if OPT.get("den", "vvvv")[c] == "v":
+            if OPT["den"][c] == "s":
                 for ps, sl in st[c]["tsum"]:
-                    nc.scalar.activation(g[:, sl], ps, ACT.Square, bias=-0.02, scale=half_w)
-                for ps, sl in st[c]["tsum"]:
-                    nc.vector.scalar_tensor_tensor(d[:, sl], ps, -half_w, g[:, sl], ALU.mult, ALU.add)
+                    nc.scalar.activation(d[:, sl], ps, ACT.Square, bias=-0.25, scale=half_w)
+                st[c]["shift"] = -0.27
             else:
-                e = work("dev%d" % c, w)
+                pm = work("pm%d" % c, w)
                 for ps, sl in st[c]["tsum"]:
-                    nc.scalar.activation(e[:, sl], ps, ACT.Square, bias=-0.52, scale=half_w)
-                nc.vector.tensor_scalar(d[:], e[:], 0.27, None, ALU.subtract)
-                st[c]["late"] = True
-            st[c]["g"] = g
+                    nc.vector.tensor_scalar(pm[:, sl], ps, half_w, 0.25, ALU.mult, ALU.add)
+                nc.vector.scalar_tensor_tensor(d[:], pm[:], 1.0, pm[:], ALU.subtract, ALU.mult)
+                st[c]["shift"] = -0.02
+                st[c]["pm"] = pm
             st[c]["den"] = d
 
         def penalty(c):
-            if "late" in st[c]:
+            w = len(chunks[c]) * P
+            g = work("pm2_%d" % c, w)
+            if OPT["pen"][c] == "s":
+                if "pm" in st[c]:
+                    nc.scalar.activation(g[:], st[c]["pm"][:], ACT.Square)
+                else:
+                    for ps, sl in st[c]["tsum"]:
+                        nc.scalar.activation(g[:, sl], ps, ACT.Square, bias=0.25, scale=half_w)
+            elif "pm" in st[c]:
+                nc.vector.tensor_tensor(g[:], st[c]["pm"][:], st[c]["pm"][:], ALU.mult)
+            else:
                 for ps, sl in st[c]["tsum"]:
-                    nc.scalar.activation(st[c]["g"][:, sl], ps, ACT.Square, bias=-0.02, scale=half_w)
+                    nc.vector.scalar_tensor_tensor(g[:, sl], ps, half_w, st[c]["den"][:, sl], ALU.mult, ALU.add)
+            st[c]["g"] = g
 
         def inverse(c):
             w = len(chunks[c]) * P
-            depth = OPT.get("depth", [2] * 4)[c]
-            prods = [st[c]["den"]]
-            for lv in range(1, depth + 1):
-                p = work("p%d_%d" % (lv, c), w >> lv)
-                nc.vector.tensor_tensor(p[:], prods[-1][:, 0 : w >> lv], prods[-1][:, w >> lv : w >> (lv - 1)], ALU.mult)
-                prods.append(p)
-            r = work("r%d_%d" % (depth, c), w >> depth)
-            nc.vector.reciprocal(r[:], prods[depth][:])
-            for lv in range(depth - 1, 0, -1):
-                nr = work("r%d_%d" % (lv, c), w >> lv)
-                nc.vector.tensor_tensor(two(nr[:]), two(prods[lv][:])[:, ::-1, :], r[:].unsqueeze(1).to_broadcast([P, 2, w >> (lv + 1)]), ALU.mult)
-                r = nr
-            st[c]["r"] = r
+            rs = work("rs%d" % c, w, "u%d_1" % (len(chunks) - 1) if c == 0 else None)
+            nc.scalar.activation(rs[:], st[c]["den"][:], ACT.Abs_reciprocal_sqrt, bias=st[c]["shift"])
+            st[c]["rs"] = rs
+
+        def squared(c):
+            w = len(chunks[c]) * P
+            if OPT["inv"][c] == "s":
+                r = work("r%d" % c, w)
+                nc.scalar.activation(r[:], st[c]["rs"][:], ACT.Square)
+                st[c]["rs"] = r
 
         def finish(c):
             w = len(chunks[c]) * P
             j0 = chunks[c][0] * P
-            if OPT.get("fold", "nnnn")[c] == "y":
-                pen = work("pen%d" % c, w)
-                nc.vector.scalar_tensor_tensor(pen[:], st[c]["g"][:], neg_brier[:, 0:1], st[c]["den"][:], ALU.mult, ALU.mult)
-                top = work("top%d" % c, w)
-                for ps, sl in st[c]["qsum"]:
-                    nc.vector.scalar_tensor_tensor(top[:, sl], ps, 0.25 * WSUM, pen[:, sl], ALU.subtract, ALU.add)
-                num = work("num%d" % c, w)
-                nc.vector.tensor_tensor(two(num[:]), two(top[:]), two(st[c]["den"][:])[:, ::-1, :], ALU.mult)
-                res = work("res%d" % c, w)
-                nc.vector.tensor_tensor(two(res[:]), two(num[:]), st[c]["r"][:].unsqueeze(1).to_broadcast([P, 2, w // 2]), ALU.mult)
-                nc.sync.dma_start(out=out[:, j0 : j0 + w], in_=res[:])
-                return
             num = work("num%d" % c, w)
-            swapped = two(st[c]["den"][:])[:, ::-1, :]
-            if len(st[c]["qsum"]) == 1:
-                nc.vector.scalar_tensor_tensor(two(num[:]), two(st[c]["qsum"][0][0]), 0.25 * WSUM, swapped, ALU.subtract, ALU.mult)
-            else:
-                for i, (ps, sl) in enumerate(st[c]["qsum"]):
-                    nc.vector.scalar_tensor_tensor(num[:, sl], ps, 0.25 * WSUM, swapped[:, i, :], ALU.subtract, ALU.mult)
-            ratio = work("ratio%d" % c, w)
-            nc.vector.tensor_tensor(two(ratio[:]), two(num[:]), st[c]["r"][:].unsqueeze(1).to_broadcast([P, 2, w // 2]), ALU.mult)
+            for ps, sl in st[c]["qsum"]:
+                nc.vector.scalar_tensor_tensor(num[:, sl], ps, 0.25 * WSUM, st[c]["rs"][:, sl], ALU.subtract, ALU.mult)
+            if OPT["inv"][c] == "v":
+                ratio = work("ratio%d" % c, w)
+                nc.vector.tensor_tensor(ratio[:], num[:], st[c]["rs"][:], ALU.mult)
+                num = ratio
             res = work("res%d" % c, w)
-            nc.vector.scalar_tensor_tensor(res[:], st[c]["g"][:], neg_brier[:, 0:1], ratio[:], ALU.mult, ALU.add)
-            j0 = chunks[c][0] * P
+            nc.vector.scalar_tensor_tensor(res[:], st[c]["g"][:], neg_brier[:, 0:1], num[:], ALU.mult, ALU.subtract)
             nc.sync.dma_start(out=out[:, j0 : j0 + w], in_=res[:])
 
-        steps = {"a": magnitude, "m": mean, "s": softplus, "n": nodes, "t": tsum, "q": squares, "d": denominator, "i": inverse, "f": finish, "p": penalty, "x": lambda c: square(c, 0), "y": lambda c: square(c, 1)}
+        steps = {"a": magnitude, "m": mean, "s": softplus, "n": nodes, "t": tsum, "q": squares, "d": denominator, "i": inverse, "f": finish, "p": penalty, "r": squared, "x": lambda c: square(c, 0), "y": lambda c: square(c, 1)}
         for word in OPT.get("order", "a0 s0 C m0 a1 m1 s1 n0 t0 n1 t1 d0 q0 d1 q1 i0 i1 f0 f1").split():
             if word == "C":
                 columns()

import math
from contextlib import ExitStack

import concourse.mybir as mybir

K, T, S, N = 512, 2048, 512, 128
FLOPS = 2 * 2 * K * S * N

F32 = mybir.dt.float32
BF16 = mybir.dt.bfloat16
I32 = mybir.dt.int32
U32 = mybir.dt.uint32
U16 = mybir.dt.uint16
U8 = mybir.dt.uint8
FP8X4 = mybir.dt.float8_e4m3fn_x4
ALU = mybir.AluOpType
ACT = mybir.ActivationFunctionType

P = 128
PACK = 4
BLOCKS = S // P
HALF = S // 2
OPT = {"order":"a0 s0 C m0 a1 s1 m1 n0 t0 d0 n1 t1 d1 i0 i1 r0 r1 q0 q1 p0 p1 f0 f1","relu":"vv","den":"ss","sq":"vvvv","pen":"vv","inv":"ss","sbanks":[4,5,6,6],"tbanks":[0,1,4,5],"qbanks":[2,2,3,7]}

NODES = (2.3344, 0.7420)
WEIGHTS = (0.0459, 0.4541)
WSUM = 0.0459 + 0.4541 + 0.4541 + 0.0459

SP_AMP = (-1.2762599117001776, -0.5435210914270948, -0.2205511065976243)
SP_SLOPE = (0.5012841530723693, 0.4992542937611325, 0.5002126802985076)
SP_SHIFT = (1.2838935200381207, 0.45991611173218133, 0.08656906098645972)
SP_BASE = 2.040332108721264


def tile_picked_yghqlr_var_p_kernel(tc, x_words, x_scales, w1, w2, offset, lab, brier, offs, out):
    nc = tc.nc
    with ExitStack() as ctx:
        keep = ctx.enter_context(tc.tile_pool(name="keep", bufs=1))
        late = ctx.enter_context(tc.tile_pool(name="late", bufs=1))
        psum = ctx.enter_context(tc.psum_pool(name="psum", bufs=1))

        def bank(i, name):
            return psum.tile([P, 512], F32, tag="bank%d" % i, name=name)

        def work(name, width, tag=None):
            return keep.tile([P, width], F32, name=name, tag=tag or name, align_bytes=64)

        chunks = OPT.get("chunks", [[0, 1], [2, 3]])
        offsets = keep.tile([P, S // 16], U16, name="offsets")
        nc.sync.dma_start(offsets[:], offs)

        raw2 = keep.tile([P, PACK, N], F32, name="raw2")
        nc.sync.dma_start(out=raw2[:], in_=w2.rearrange("(p j) n -> p j n", j=PACK))

        ones = late.tile([P, P], F32, name="ones", offset=4 * T - 64, align_bytes=64)
        nc.gpsimd.memset(ones[:], 1.0)
        scale_tab = keep.tile([P, T], U8, name="scale_tab", align_bytes=64)
        nc.gpsimd.memset(scale_tab[:].bitcast(I32), 0)
        for q in range(4):
            nc.sync.dma_start(out=scale_tab[32 * q : 32 * q + 4, :].bitcast(I32), in_=x_scales[0, 4 * q : 4 * q + 4, :].bitcast(I32))

        ident = keep.tile([P, P], F32, name="ident")
        nc.gpsimd.affine_select(out=ident[:], in_=ones[:], compare_op=ALU.is_equal, fill=0.0, base=0, pattern=[[-1, P]], channel_multiplier=1)
        word_tab = late.tile([P, T], I32, name="word_tab", offset=0, align_bytes=64)
        nc.sync.dma_start(out=word_tab[:], in_=x_words[0].rearrange("p n t -> p (n t)").bitcast(I32))

        raw1 = late.tile([P, PACK, N], F32, name="raw1", offset=4 * T + 4 * P - 128, align_bytes=64)
        nc.sync.dma_start(out=raw1[:], in_=w1.rearrange("(p j) n -> p j n", j=PACK))

        rows = keep.tile([P, P], F32, name="rows")
        nc.gpsimd.memset(rows[:], 0.0)
        nc.sync.dma_start(out=rows[0:BLOCKS, :], in_=offset[0].rearrange("(b p) -> b p", p=P))
        nc.sync.dma_start(out=rows[32 : 32 + BLOCKS, :], in_=lab[0].rearrange("(b p) -> b p", p=P))
        nc.sync.dma_start(out=rows[64:65, :], in_=brier.rearrange("p o -> o p"))

        def quantised(raw, cast, name):
            grouped = keep.tile([P, N, PACK], BF16, name=name + "_grouped", align_bytes=64)
            cast(grouped[:], raw[:].rearrange("p j n -> p n j"))
            codes = keep.tile([P, N], U32, name=name + "_codes", align_bytes=64)
            scale = keep.tile([P, N], U8, name=name + "_scale", align_bytes=64)
            nc.vector.quantize_mx(out=codes[:].bitcast(FP8X4), scales=scale[:], in_=grouped[:].rearrange("p n j -> p (n j)"))
            return codes, scale

        w2q = quantised(raw2, nc.vector.tensor_copy, "w2")

        x_scale, x_codes = [], []
        for h in range(2):
            sc = keep.tile([P, HALF], U8, name="x_scale%d" % h, align_bytes=64)
            nc.vector.tensor_copy(sc[:], scale_tab[:].indirect(offsets[:, h * HALF // 16 : (h + 1) * HALF // 16]))
            x_scale.append(sc)
        for h in range(2):
            co = keep.tile([P, HALF], U32, name="x_codes%d" % h, align_bytes=64)
            nc.vector.tensor_copy(co[:], word_tab[:].bitcast(U32).indirect(offsets[:, h * HALF // 16 : (h + 1) * HALF // 16]))
            x_codes.append(co)

        def product(acc, col, b, wq):
            j0 = (b % 2) * P
            nc.tensor.matmul_mx(
                out=acc[:, col * P : (col + 1) * P],
                lhsT=x_codes[b // 2][:, j0 : j0 + P].bitcast(FP8X4),
                lhsT_scale=x_scale[b // 2][:, j0 : j0 + P],
                rhs=wq[0][:].bitcast(FP8X4),
                rhs_scale=wq[1][:],
                start=True,
                stop=True,
            )

        ys, ym = [], []
        for h in range(2):
            acc = bank(h, "ys%d" % h)
            nc.tensor.matmul_mx(
                out=acc[:, 0:HALF],
                lhsT=w2q[0][:].bitcast(FP8X4),
                lhsT_scale=w2q[1][:],
                rhs=x_codes[h][:].bitcast(FP8X4),
                rhs_scale=x_scale[h][:],
                start=True,
                stop=True,
            )
            ys.append(acc)
        w1q = quantised(raw1, nc.scalar.copy if OPT.get("cast1", "s") == "s" else nc.vector.tensor_copy, "w1")
        for h in range(2):
            acc = bank(2 + h, "ym%d" % h)
            for b in range(2):
                product(acc, b, 2 * h + b, w1q)
            ym.append(acc)
            if h == 0:
                cols = acc[:, HALF : HALF + P]
                nc.tensor.transpose(cols, rows[:], ident[:])
        off_col = keep.tile([P, BLOCKS], F32, name="off_col")
        flip_col = keep.tile([P, BLOCKS], F32, name="flip_col")
        neg_brier = keep.tile([P, 1], F32, name="neg_brier")

        def two(ap):
            return ap.rearrange("p (u c) -> p u c", u=2)

        half_w = 0.5 * WEIGHTS[1]
        lift = (0.5 * WSUM - 0.25) / half_w
        st = [dict() for c in chunks]
        sbanks = OPT.get("sbanks", [4, 4, 5, 5])
        tbanks = OPT.get("tbanks", [6, 7, 0, 1])
        qbanks = OPT.get("qbanks", [2, 2, 3, 3])

        def view(banks, c):
            b0 = chunks[c][0]
            return banks[b0 // 2][:, (b0 % 2) * P : (b0 % 2 + len(chunks[c])) * P]

        def magnitude(c):
            w = len(chunks[c]) * P
            st[c]["mag"] = work("mag%d" % c, w)
            nc.scalar.activation(st[c]["mag"][:], view(ys, c), ACT.Abs)
            st[c]["acc"] = work("relu%d" % c, w)
            if OPT.get("relu", "vvvv")[c] == "v":
                nc.vector.tensor_scalar(st[c]["acc"][:], view(ys, c), 0.0, -1.0 / SP_AMP[0], ALU.max, ALU.mult)
            else:
                nc.scalar.activation(st[c]["acc"][:], view(ys, c), ACT.Relu, scale=-1.0 / SP_AMP[0])

        def columns():
            nc.vector.tensor_copy(off_col[:], cols[:, 0:BLOCKS])
            nc.vector.tensor_scalar(flip_col[:], cols[:, 32 : 32 + BLOCKS], -2.0, 1.0, ALU.mult, ALU.add)
            nc.vector.tensor_scalar(neg_brier[:], cols[:, 64:65], -1.0, None, ALU.mult)

        def mean(c):
            a = work("mean%d" % c, len(chunks[c]) * P)
            for i, b in enumerate(chunks[c]):
                nc.vector.tensor_scalar(a[:, i * P : (i + 1) * P], ym[b // 2][:, (b % 2) * P : (b % 2 + 1) * P], off_col[:, b : b + 1], flip_col[:, b : b + 1], ALU.add, ALU.mult)
            st[c]["mean"] = a

        def softplus(c):
            w = len(chunks[c]) * P
            addends = [st[c]["acc"][:]]
            for i in (2, 1, 0):
                g = work("g%d_%d" % (c, i), w)
                nc.scalar.activation(g[:], st[c]["mag"][:], ACT.Tanh, bias=-SP_SHIFT[i], scale=-SP_SLOPE[i])
                if i:
                    s = work("gs%d_%d" % (c, i), w)
                    nc.vector.tensor_scalar(s[:], g[:], SP_AMP[i] / SP_AMP[0], None, ALU.mult)
                    g = s
                addends.append(g[:])
            st[c]["ssum"] = summed(c, addends, sbanks, "ssum")

        def nodes(c):
            w = len(chunks[c]) * P
            ts = []
            for node in range(2):
                u = work("u%d_%d" % (c, node), 2 * w)
                t = work("t%d_%d" % (c, node), 2 * w)
                for i, sign in enumerate((1.0, -1.0)):
                    for ps, sl in st[c]["ssum"]:
                        nc.vector.scalar_tensor_tensor(u[:, i * w : (i + 1) * w][:, sl], ps, -0.8 * SP_AMP[0] * sign * NODES[node], st[c]["mean"][:, sl], ALU.mult, ALU.add)
                    nc.scalar.activation(t[:, i * w : (i + 1) * w], u[:, i * w : (i + 1) * w], ACT.Tanh, bias=0.5 * sign * NODES[node] * (0.8 * SP_BASE + 0.3), scale=0.5)
                ts.append(t)
            st[c]["t"] = ts

        def summed(c, addends, ids, name):
            w = len(chunks[c]) * P
            tiles = {}
            for b in chunks[c]:
                if ids[b] not in tiles:
                    tiles[ids[b]] = bank(ids[b], "%s%d_%d" % (name, c, b))
            shared = len(tiles) == 1
            outs = [tiles[ids[b]][:, (i * P if shared else 0) : (i * P if shared else 0) + P] for i, b in enumerate(chunks[c])]
            order = [(i, k) for i in range(len(outs)) for k in range(4)] if shared else [(i, k) for k in range(4) for i in range(len(outs))]
            for i, k in order:
                nc.tensor.matmul(outs[i], addends[k][:, i * P : (i + 1) * P], ident[:], start=(k == 0), stop=(k == 3), is_transpose=True)
            if shared:
                return [(tiles[ids[chunks[c][0]]][:, 0:w], slice(0, w))]
            return [(outs[i], slice(i * P, (i + 1) * P)) for i in range(len(outs))]

        def tsum(c):
            w = len(chunks[c]) * P
            s = work("ts%d" % c, 2 * w)
            if OPT.get("ts", "vvvv")[c] == "v":
                nc.vector.tensor_scalar(s[:], st[c]["t"][0][:], WEIGHTS[0] / WEIGHTS[1], 0.5 * lift, ALU.mult, ALU.add)
            elif OPT.get("ts")[c] == "g":
                nc.gpsimd.tensor_scalar(s[:], st[c]["t"][0][:], WEIGHTS[0] / WEIGHTS[1], 0.5 * lift, ALU.mult, ALU.add)
            else:
                nc.scalar.activation(s[:], st[c]["t"][0][:], ACT.Identity, bias=0.5 * lift, scale=WEIGHTS[0] / WEIGHTS[1])
            st[c]["tsum"] = summed(c, [x[:, k * w : (k + 1) * w] for x in (s, st[c]["t"][1]) for k in range(2)], tbanks, "tsum")

        def square(c, node):
            w = len(chunks[c]) * P
            sq = work("sq%d_%d" % (c, node), 2 * w, OPT.get("sqtag", {}).get("%d%d" % (c, node)))
            t = st[c]["t"][node]
            mode = OPT.get("sq", "ssssssss")[2 * c + node]
            for sl in [slice(0, 2 * w)] if mode in "sv" else [slice(0, w), slice(w, 2 * w)]:
                if mode in "sS":
                    nc.scalar.activation(sq[:, sl], t[:, sl], ACT.Square, scale=0.5 * math.sqrt(WEIGHTS[node]))
                else:
                    nc.vector.scalar_tensor_tensor(sq[:, sl], t[:, sl], 0.25 * WEIGHTS[node], t[:, sl], ALU.mult, ALU.mult)
            st[c]["sq%d" % node] = sq

        def squares(c):
            w = len(chunks[c]) * P
            for node in range(2):
                if "sq%d" % node not in st[c]:
                    square(c, node)
            sqs = [st[c]["sq0"], st[c]["sq1"]]
            st[c]["qsum"] = summed(c, [x[:, k * w : (k + 1) * w] for x in sqs for k in range(2)], qbanks, "qsum")

        def denominator(c):
            w = len(chunks[c]) * P
            d = work("den%d" % c, w)
            if OPT["den"][c] == "s":
                for ps, sl in st[c]["tsum"]:
                    nc.scalar.activation(d[:, sl], ps, ACT.Square, bias=-0.25, scale=half_w)
                st[c]["shift"] = -0.27
            else:
                pm = work("pm%d" % c, w)
                for ps, sl in st[c]["tsum"]:
                    nc.vector.tensor_scalar(pm[:, sl], ps, half_w, 0.25, ALU.mult, ALU.add)
                nc.vector.scalar_tensor_tensor(d[:], pm[:], 1.0, pm[:], ALU.subtract, ALU.mult)
                st[c]["shift"] = -0.02
                st[c]["pm"] = pm
            st[c]["den"] = d

        def penalty(c):
            w = len(chunks[c]) * P
            g = work("pm2_%d" % c, w)
            if OPT["pen"][c] == "s":
                if "pm" in st[c]:
                    nc.scalar.activation(g[:], st[c]["pm"][:], ACT.Square)
                else:
                    for ps, sl in st[c]["tsum"]:
                        nc.scalar.activation(g[:, sl], ps, ACT.Square, bias=0.25, scale=half_w)
            elif "pm" in st[c]:
                nc.vector.tensor_tensor(g[:], st[c]["pm"][:], st[c]["pm"][:], ALU.mult)
            else:
                for ps, sl in st[c]["tsum"]:
                    nc.vector.scalar_tensor_tensor(g[:, sl], ps, half_w, st[c]["den"][:, sl], ALU.mult, ALU.add)
            st[c]["g"] = g

        def inverse(c):
            w = len(chunks[c]) * P
            rs = work("rs%d" % c, w, "u%d_1" % (len(chunks) - 1) if c == 0 else None)
            nc.scalar.activation(rs[:], st[c]["den"][:], ACT.Abs_reciprocal_sqrt, bias=st[c]["shift"])
            st[c]["rs"] = rs

        def squared(c):
            w = len(chunks[c]) * P
            if OPT["inv"][c] == "s":
                r = work("r%d" % c, w)
                nc.scalar.activation(r[:], st[c]["rs"][:], ACT.Square)
                st[c]["rs"] = r

        def finish(c):
            w = len(chunks[c]) * P
            j0 = chunks[c][0] * P
            num = work("num%d" % c, w)
            for ps, sl in st[c]["qsum"]:
                nc.vector.scalar_tensor_tensor(num[:, sl], ps, 0.25 * WSUM, st[c]["rs"][:, sl], ALU.subtract, ALU.mult)
            if OPT["inv"][c] == "v":
                ratio = work("ratio%d" % c, w)
                nc.vector.tensor_tensor(ratio[:], num[:], st[c]["rs"][:], ALU.mult)
                num = ratio
            res = work("res%d" % c, w)
            nc.vector.scalar_tensor_tensor(res[:], st[c]["g"][:], neg_brier[:, 0:1], num[:], ALU.mult, ALU.subtract)
            nc.sync.dma_start(out=out[:, j0 : j0 + w], in_=res[:])

        steps = {"a": magnitude, "m": mean, "s": softplus, "n": nodes, "t": tsum, "q": squares, "d": denominator, "i": inverse, "f": finish, "p": penalty, "r": squared, "x": lambda c: square(c, 0), "y": lambda c: square(c, 1)}
        for word in OPT.get("order", "a0 s0 C m0 a1 m1 s1 n0 t0 n1 t1 d0 q0 d1 q1 i0 i1 f0 f1").split():
            if word == "C":
                columns()
            else:
                steps[word[0]](int(word[1]))
